import numpy as np
CORES = [74,78,202,206,330,334,458,462]
N = 8
def setup_inputs(rng):
    return {"x": rng.standard_normal((N, 128, 128), dtype=np.float32)}
def reference(x):
    g = np.concatenate(list(x), axis=1)
    return {"y": np.broadcast_to(g, (N,) + g.shape)}

@@ -1,0 +1,82 @@
+from concourse.bass import DstId, RemoteDMATransfer
+
+SCRATCH = {
+    "land": ("dram", [16, 128, 64], "float32"),
+}
+SEMAPHORES = ["ld", "go", "sent", "st_sync", "st_scal"] + ["p%d" % i for i in range(16)]
+
+RANK_CORES = (2, 6)
+CABLE_HELPER = {2: 0, 6: 4}
+SWITCH_HELPER = {2: 3, 6: 7}
+
+
+def rank_program(g, core, T, topo):
+    chip_base = (T.cores[0] % 128) // 8 * 8
+    if topo.chip(core) * 8 != chip_base:
+        return
+    h, k = topo.host(core), core % 8
+
+    def at(host, kk):
+        return 128 * host + chip_base + kk
+
+    def slot(host, c, half):
+        return 2 * T.rank_of(at(host, c)) + half
+
+    def xfer(p, dsts, mask):
+        ids = []
+        for d in dsts:
+            rid, pid = topo.addr(d, core)
+            ids.append(DstId(rid=rid, pnc=pid))
+        return RemoteDMATransfer(dst_ids=ids, dma_engine_mask=mask, remote_sem=T.sem["p%d" % p],
+                                 srcs=[T.land[p]], dsts=[T.land[p] for _ in dsts], alu_op=0)
+
+    hs, hc, hd = h ^ 1, 3 - h, (h + 2) % 4
+
+    if k in RANK_CORES:
+        j = T.rank_of(core)
+        a, b = 2 * j, 2 * j + 1
+        mate = at(h, 8 - k)
+        g.sync.dma_start(T.land[a:a + 2], T.x[:, :]).then_inc(T.sem.ld, 16)
+        g.wait_ge(T.sem.ld, 16)
+        g.remote_dma_fused([xfer(a, [at(hs, CABLE_HELPER[k])], 0x000F),
+                            xfer(b, [at(hc, SWITCH_HELPER[k])], 0x00F0)], local_sem=T.sem.sent)
+        g.remote_dma_fused([xfer(b, [at(hs, 2), at(hs, 6)], 0x000F),
+                            xfer(a, [at(hc, 2), at(hc, 6)], 0x00F0),
+                            xfer(a, [mate], 0x0F00),
+                            xfer(b, [mate], 0xF000)], local_sem=T.sem.sent)
+        g.sem_inc(T.sem.go, 1)
+
+        def store(q, sem, host, c, need):
+            r = T.rank_of(at(host, c))
+            for half in (0, 1):
+                q.wait_ge(T.sem["p%d" % (2 * r + half)], need[half])
+            q.dma_start(T.y[:, 128 * r:128 * r + 128], T.land[2 * r:2 * r + 2]).then_inc(sem, 16)
+
+        sy, sc = g.sync, g.scalar
+        store(sy, T.sem.st_sync, h, 8 - k, (4, 4))
+        store(sy, T.sem.st_sync, hs, 2, (8, 4))
+        store(sy, T.sem.st_sync, hs, 6, (8, 4))
+        store(sy, T.sem.st_sync, hd, 2, (8, 8))
+        sy.wait_ge(T.sem.st_sync, 64)
+
+        sc.wait_ge(T.sem.go, 1)
+        sc.dma_start(T.y[:, 128 * j:128 * j + 128], T.x[:, :]).then_inc(T.sem.st_scal, 16)
+        store(sc, T.sem.st_scal, hc, 2, (4, 8))
+        store(sc, T.sem.st_scal, hc, 6, (4, 8))
+        store(sc, T.sem.st_scal, hd, 6, (8, 8))
+        sc.wait_ge(T.sem.st_scal, 64)
+
+        g.wait_ge(T.sem.sent, 24)
+        return
+
+    for c in RANK_CORES:
+        if k == CABLE_HELPER[c]:
+            p, nxt = slot(hs, c, 0), hc
+        elif k == SWITCH_HELPER[c]:
+            p, nxt = slot(hc, c, 1), hs
+        else:
+            continue
+        g.wait_ge(T.sem["p%d" % p], 4)
+        g.remote_dma_fused([xfer(p, [at(nxt, 2), at(nxt, 6)], 0x00FF),
+                            xfer(p, [at(h, 2), at(h, 6)], 0xFF00)], local_sem=T.sem.sent)
+        g.wait_ge(T.sem.sent, 16)

@@ -41,29 +41,30 @@ def rank_program(g, core, T, topo):
         g.remote_dma_fused([xfer(a, [at(hs, CABLE_HELPER[k])], 0x000F),
                             xfer(b, [at(hc, SWITCH_HELPER[k])], 0x00F0)], local_sem=T.sem.sent)
         g.remote_dma_fused([xfer(b, [at(hs, 2), at(hs, 6)], 0x000F),
-                            xfer(a, [at(hc, 2), at(hc, 6)], 0x00F0),
+                            xfer(a, [at(hc, SWITCH_HELPER[k])], 0x00F0),
                             xfer(a, [mate], 0x0F00),
                             xfer(b, [mate], 0xF000)], local_sem=T.sem.sent)
         g.sem_inc(T.sem.go, 1)
 
-        def store(q, sem, host, c, need):
+        def store(q, sem, host, c, halves, need):
             r = T.rank_of(at(host, c))
-            for half in (0, 1):
-                q.wait_ge(T.sem["p%d" % (2 * r + half)], need[half])
-            q.dma_start(T.y[:, 128 * r:128 * r + 128], T.land[2 * r:2 * r + 2]).then_inc(sem, 16)
+            for half, n in zip(halves, need):
+                q.wait_ge(T.sem["p%d" % (2 * r + half)], n)
+            lo, hi = halves[0], halves[-1] + 1
+            q.dma_start(T.y[64 * lo:64 * hi, 128 * r:128 * r + 128], T.land[2 * r + lo:2 * r + hi]).then_inc(sem, 16)
 
         sy, sc = g.sync, g.scalar
-        store(sy, T.sem.st_sync, h, 8 - k, (4, 4))
-        store(sy, T.sem.st_sync, hs, 2, (8, 4))
-        store(sy, T.sem.st_sync, hs, 6, (8, 4))
-        store(sy, T.sem.st_sync, hd, 2, (8, 8))
+        store(sy, T.sem.st_sync, h, 8 - k, (0, 1), (4, 4))
+        store(sy, T.sem.st_sync, hs, 2, (0, 1), (8, 4))
+        store(sy, T.sem.st_sync, hs, 6, (0, 1), (8, 4))
+        store(sy, T.sem.st_sync, hd, 2, (0, 1), (8, 8))
         sy.wait_ge(T.sem.st_sync, 64)
 
         sc.wait_ge(T.sem.go, 1)
         sc.dma_start(T.y[:, 128 * j:128 * j + 128], T.x[:, :]).then_inc(T.sem.st_scal, 16)
-        store(sc, T.sem.st_scal, hc, 2, (4, 8))
-        store(sc, T.sem.st_scal, hc, 6, (4, 8))
-        store(sc, T.sem.st_scal, hd, 6, (8, 8))
+        store(sc, T.sem.st_scal, hc, 2, (0, 1), (8, 8))
+        store(sc, T.sem.st_scal, hc, 6, (0, 1), (8, 8))
+        store(sc, T.sem.st_scal, hd, 6, (0, 1), (8, 8))
         sc.wait_ge(T.sem.st_scal, 64)
 
         g.wait_ge(T.sem.sent, 24)
@@ -71,12 +72,16 @@ def rank_program(g, core, T, topo):
 
     for c in RANK_CORES:
         if k == CABLE_HELPER[c]:
-            p, nxt = slot(hs, c, 0), hc
+            p = slot(hs, c, 0)
+            g.wait_ge(T.sem["p%d" % p], 4)
+            g.remote_dma_fused([xfer(p, [at(hc, 2), at(hc, 6)], 0x00FF),
+                                xfer(p, [at(h, 2), at(h, 6)], 0xFF00)], local_sem=T.sem.sent)
+            g.wait_ge(T.sem.sent, 16)
         elif k == SWITCH_HELPER[c]:
-            p, nxt = slot(hc, c, 1), hs
-        else:
-            continue
-        g.wait_ge(T.sem["p%d" % p], 4)
-        g.remote_dma_fused([xfer(p, [at(nxt, 2), at(nxt, 6)], 0x00FF),
-                            xfer(p, [at(h, 2), at(h, 6)], 0xFF00)], local_sem=T.sem.sent)
-        g.wait_ge(T.sem.sent, 16)
+            p, pa = slot(hc, c, 1), slot(hc, c, 0)
+            g.wait_ge(T.sem["p%d" % p], 4)
+            g.remote_dma_fused([xfer(p, [at(hs, 2), at(hs, 6)], 0x00FF),
+                                xfer(p, [at(h, 2), at(h, 6)], 0xFF00)], local_sem=T.sem.sent)
+            g.wait_ge(T.sem["p%d" % pa], 4)
+            g.remote_dma_fused([xfer(pa, [at(h, 2), at(h, 6)], 0xFF00)], local_sem=T.sem.sent)
+            g.wait_ge(T.sem.sent, 24)

@@ -7,6 +7,7 @@ SEMAPHORES = ["ld", "go", "sent", "st_sync", "st_scal"] + ["p%d" % i for i in ra
 
 RANK_CORES = (2, 6)
 CABLE_HELPER = {2: 0, 6: 4}
+FAN_HELPER = {2: 1, 6: 5}
 SWITCH_HELPER = {2: 3, 6: 7}
 
 
@@ -57,14 +58,14 @@ def rank_program(g, core, T, topo):
         store(sy, T.sem.st_sync, h, 8 - k, (0, 1), (4, 4))
         store(sy, T.sem.st_sync, hs, 2, (0, 1), (8, 4))
         store(sy, T.sem.st_sync, hs, 6, (0, 1), (8, 4))
-        store(sy, T.sem.st_sync, hd, 2, (0, 1), (8, 8))
+        store(sy, T.sem.st_sync, hd, 2, (0, 1), (16, 8))
         sy.wait_ge(T.sem.st_sync, 64)
 
         sc.wait_ge(T.sem.go, 1)
         sc.dma_start(T.y[:, 128 * j:128 * j + 128], T.x[:, :]).then_inc(T.sem.st_scal, 16)
         store(sc, T.sem.st_scal, hc, 2, (0, 1), (8, 8))
         store(sc, T.sem.st_scal, hc, 6, (0, 1), (8, 8))
-        store(sc, T.sem.st_scal, hd, 6, (0, 1), (8, 8))
+        store(sc, T.sem.st_scal, hd, 6, (0, 1), (16, 8))
         sc.wait_ge(T.sem.st_scal, 64)
 
         g.wait_ge(T.sem.sent, 24)
@@ -74,8 +75,13 @@ def rank_program(g, core, T, topo):
         if k == CABLE_HELPER[c]:
             p = slot(hs, c, 0)
             g.wait_ge(T.sem["p%d" % p], 4)
-            g.remote_dma_fused([xfer(p, [at(hc, 2), at(hc, 6)], 0x00FF),
+            g.remote_dma_fused([xfer(p, [at(hc, FAN_HELPER[c])], 0x00FF),
                                 xfer(p, [at(h, 2), at(h, 6)], 0xFF00)], local_sem=T.sem.sent)
+            g.wait_ge(T.sem.sent, 16)
+        elif k == FAN_HELPER[c]:
+            p = slot(hd, c, 0)
+            g.wait_ge(T.sem["p%d" % p], 8)
+            g.remote_dma_fused([xfer(p, [at(h, 2), at(h, 6)], 0xFFFF)], local_sem=T.sem.sent)
             g.wait_ge(T.sem.sent, 16)
         elif k == SWITCH_HELPER[c]:
             p, pa = slot(hc, c, 1), slot(hc, c, 0)

@@ -58,15 +58,19 @@ def rank_program(g, core, T, topo):
         store(sy, T.sem.st_sync, h, 8 - k, (0, 1), (4, 4))
         store(sy, T.sem.st_sync, hs, 2, (0, 1), (8, 4))
         store(sy, T.sem.st_sync, hs, 6, (0, 1), (8, 4))
-        store(sy, T.sem.st_sync, hd, 2, (0, 1), (16, 8))
-        sy.wait_ge(T.sem.st_sync, 64)
+        store(sy, T.sem.st_sync, hd, 2, (1,), (8,))
+        store(sy, T.sem.st_sync, hd, 6, (1,), (8,))
+        store(sy, T.sem.st_sync, hd, 2, (0,), (16,))
+        store(sy, T.sem.st_sync, hd, 6, (0,), (16,))
+        sy.wait_ge(T.sem.st_sync, 112)
 
         sc.wait_ge(T.sem.go, 1)
         sc.dma_start(T.y[:, 128 * j:128 * j + 128], T.x[:, :]).then_inc(T.sem.st_scal, 16)
-        store(sc, T.sem.st_scal, hc, 2, (0, 1), (8, 8))
-        store(sc, T.sem.st_scal, hc, 6, (0, 1), (8, 8))
-        store(sc, T.sem.st_scal, hd, 6, (0, 1), (16, 8))
-        sc.wait_ge(T.sem.st_scal, 64)
+        store(sc, T.sem.st_scal, hc, 2, (1,), (8,))
+        store(sc, T.sem.st_scal, hc, 6, (1,), (8,))
+        store(sc, T.sem.st_scal, hc, 2, (0,), (8,))
+        store(sc, T.sem.st_scal, hc, 6, (0,), (8,))
+        sc.wait_ge(T.sem.st_scal, 80)
 
         g.wait_ge(T.sem.sent, 24)
         return

from concourse.bass import DstId, RemoteDMATransfer

SCRATCH = {
    "land": ("dram", [16, 128, 64], "float32"),
}
SEMAPHORES = ["ld", "go", "sent", "st_sync", "st_scal"] + ["p%d" % i for i in range(16)]

RANK_CORES = (2, 6)
CABLE_HELPER = {2: 0, 6: 4}
FAN_HELPER = {2: 1, 6: 5}
SWITCH_HELPER = {2: 3, 6: 7}


def rank_program(g, core, T, topo):
    chip_base = (T.cores[0] % 128) // 8 * 8
    if topo.chip(core) * 8 != chip_base:
        return
    h, k = topo.host(core), core % 8

    def at(host, kk):
        return 128 * host + chip_base + kk

    def slot(host, c, half):
        return 2 * T.rank_of(at(host, c)) + half

    def xfer(p, dsts, mask):
        ids = []
        for d in dsts:
            rid, pid = topo.addr(d, core)
            ids.append(DstId(rid=rid, pnc=pid))
        return RemoteDMATransfer(dst_ids=ids, dma_engine_mask=mask, remote_sem=T.sem["p%d" % p],
                                 srcs=[T.land[p]], dsts=[T.land[p] for _ in dsts], alu_op=0)

    hs, hc, hd = h ^ 1, 3 - h, (h + 2) % 4

    if k in RANK_CORES:
        j = T.rank_of(core)
        a, b = 2 * j, 2 * j + 1
        mate = at(h, 8 - k)
        g.sync.dma_start(T.land[a:a + 2], T.x[:, :]).then_inc(T.sem.ld, 16)
        g.wait_ge(T.sem.ld, 16)
        g.remote_dma_fused([xfer(a, [at(hs, CABLE_HELPER[k])], 0x000F),
                            xfer(b, [at(hc, SWITCH_HELPER[k])], 0x00F0)], local_sem=T.sem.sent)
        g.remote_dma_fused([xfer(b, [at(hs, 2), at(hs, 6)], 0x000F),
                            xfer(a, [at(hc, SWITCH_HELPER[k])], 0x00F0),
                            xfer(a, [mate], 0x0F00),
                            xfer(b, [mate], 0xF000)], local_sem=T.sem.sent)
        g.sem_inc(T.sem.go, 1)

        def store(q, sem, host, c, halves, need):
            r = T.rank_of(at(host, c))
            for half, n in zip(halves, need):
                q.wait_ge(T.sem["p%d" % (2 * r + half)], n)
            lo, hi = halves[0], halves[-1] + 1
            q.dma_start(T.y[64 * lo:64 * hi, 128 * r:128 * r + 128], T.land[2 * r + lo:2 * r + hi]).then_inc(sem, 16)

        sy, sc = g.sync, g.scalar
        store(sy, T.sem.st_sync, h, 8 - k, (0, 1), (4, 4))
        store(sy, T.sem.st_sync, hs, 2, (0, 1), (8, 4))
        store(sy, T.sem.st_sync, hs, 6, (0, 1), (8, 4))
        store(sy, T.sem.st_sync, hd, 2, (1,), (8,))
        store(sy, T.sem.st_sync, hd, 6, (1,), (8,))
        store(sy, T.sem.st_sync, hd, 2, (0,), (16,))
        store(sy, T.sem.st_sync, hd, 6, (0,), (16,))
        sy.wait_ge(T.sem.st_sync, 112)

        sc.wait_ge(T.sem.go, 1)
        sc.dma_start(T.y[:, 128 * j:128 * j + 128], T.x[:, :]).then_inc(T.sem.st_scal, 16)
        store(sc, T.sem.st_scal, hc, 2, (1,), (8,))
        store(sc, T.sem.st_scal, hc, 6, (1,), (8,))
        store(sc, T.sem.st_scal, hc, 2, (0,), (8,))
        store(sc, T.sem.st_scal, hc, 6, (0,), (8,))
        sc.wait_ge(T.sem.st_scal, 80)

        g.wait_ge(T.sem.sent, 24)
        return

    for c in RANK_CORES:
        if k == CABLE_HELPER[c]:
            p = slot(hs, c, 0)
            g.wait_ge(T.sem["p%d" % p], 4)
            g.remote_dma_fused([xfer(p, [at(hc, FAN_HELPER[c])], 0x00FF),
                                xfer(p, [at(h, 2), at(h, 6)], 0xFF00)], local_sem=T.sem.sent)
            g.wait_ge(T.sem.sent, 16)
        elif k == FAN_HELPER[c]:
            p = slot(hd, c, 0)
            g.wait_ge(T.sem["p%d" % p], 8)
            g.remote_dma_fused([xfer(p, [at(h, 2), at(h, 6)], 0xFFFF)], local_sem=T.sem.sent)
            g.wait_ge(T.sem.sent, 16)
        elif k == SWITCH_HELPER[c]:
            p, pa = slot(hc, c, 1), slot(hc, c, 0)
            g.wait_ge(T.sem["p%d" % p], 4)
            g.remote_dma_fused([xfer(p, [at(hs, 2), at(hs, 6)], 0x00FF),
                                xfer(p, [at(h, 2), at(h, 6)], 0xFF00)], local_sem=T.sem.sent)
            g.wait_ge(T.sem["p%d" % pa], 4)
            g.remote_dma_fused([xfer(pa, [at(h, 2), at(h, 6)], 0xFF00)], local_sem=T.sem.sent)
            g.wait_ge(T.sem.sent, 24)
